import numpy as np
import ml_dtypes


def mxq(x, axis, fmt="e4m3"):
    dtype, down = {"e4m3": (ml_dtypes.float8_e4m3fn, 7), "e5m2": (ml_dtypes.float8_e5m2, 14)}[fmt]
    v = np.moveaxis(np.asarray(x, np.float32).astype(ml_dtypes.bfloat16).astype(np.float64), axis, -1)
    blocks = v.reshape(v.shape[:-1] + (-1, 32))
    amax = np.abs(blocks).max(-1, keepdims=True)
    byte = np.maximum(np.where(amax > 0, np.frexp(amax)[1] - 1 + 127, 0) - down, 1)
    scale = np.exp2(byte - 127.0)
    codes = (blocks / scale).astype(np.float32).astype(dtype).astype(np.float64)
    return np.moveaxis((codes * scale).reshape(v.shape), -1, axis)


WIDE = False


def mx_kscale(k):
    if not WIDE:
        return np.ones(k)
    levels = np.array([10, -10, 5, -5, 0])
    if k % 512:
        return np.exp2(np.random.permutation(np.resize(levels, k // 32))).repeat(32)
    a = np.empty((k // 512, 16))
    for p in range(k // 512):
        a[p, :8] = np.random.permutation(np.resize(levels, 8))
        for g in range(8):
            far = levels[np.abs(levels - a[p, g]) >= 10]
            a[p, g + 8] = far[np.random.randint(len(far))]
    return np.exp2(a.ravel()).repeat(32)


def f64(x):
    return np.asarray(x).astype(np.float64)


def striped(idx):
    return np.tile(idx.reshape(-1, 16).T, (8, 1)).astype(np.uint16)


def unstriped(offs):
    return offs[:16].T.reshape(-1).astype(np.int64)


E2M1 = np.array([0.0, 0.5, 1.0, 1.5, 2.0, 3.0, 4.0, 6.0, -0.0, -0.5, -1.0, -1.5, -2.0, -3.0, -4.0, -6.0])


def pack_weight(w, fmt):
    k, n = w.shape
    w = f64(np.asarray(w, np.float32).astype(ml_dtypes.bfloat16)).reshape(k // 32, 32, n)
    amax = np.abs(w).max(1)
    if fmt == "e4m3":
        byte = np.frexp(amax)[1] - 1 + 127 - 7
    else:
        mant, ex = np.frexp(amax / 6.0)
        byte = np.where(mant > 0.5, ex, ex - 1) + 127
    byte = np.clip(np.where(amax > 0, byte, 1), 1, 254)
    scaled = (w * np.exp2(127.0 - byte)[:, None, :]).reshape(k, n).astype(np.float32)
    by_word = np.ascontiguousarray(scaled.reshape(k // 512, 128, 4, n).transpose(0, 1, 3, 2))
    if fmt == "e4m3":
        words = by_word.astype(ml_dtypes.float8_e4m3fn).view(np.uint8)
    else:
        c = by_word.astype(ml_dtypes.float4_e2m1fn).view(np.uint8) & 0xF
        words = (c[..., 0::2] | (c[..., 1::2] << 4)).reshape(k // 512, 128, 2 * n)
    return np.ascontiguousarray(words), np.ascontiguousarray(byte.astype(np.uint8).reshape(k // 512, 16, n))


def unpack_weight(words, scales, fmt):
    g, _, n = scales.shape
    words = np.ascontiguousarray(words).reshape(g, 128, n, -1)
    if fmt == "e4m3":
        vals = words.view(ml_dtypes.float8_e4m3fn).astype(np.float64)
    else:
        nib = np.empty((g, 128, n, 4), np.uint8)
        nib[..., 0::2] = words & 0xF
        nib[..., 1::2] = words >> 4
        vals = E2M1[nib]
    vals = vals * np.repeat(np.exp2(scales.astype(np.float64) - 127.0), 8, axis=1)[..., None]
    return vals.transpose(0, 1, 3, 2).reshape(g * 512, n)


def gelu(v):
    return 0.5 * v * (1.0 + np.tanh(np.sqrt(2.0 / np.pi) * (v + 0.044715 * v**3)))


K, K2, H, N, T, TB, S, T2 = 512, 1024, 512, 768, 2048, 1024, 512, 1024

def setup_inputs():
    n = np.random.standard_normal
    s, s2, u = mx_kscale(K)[:, None], mx_kscale(K2)[:, None], mx_kscale(H)[:, None]
    tab_words, tab_scales = pack_weight(n((K, T)) * s, "e4m3")
    tab2_words, tab2_scales = pack_weight(n((K2, TB)) * s2, "e4m3")
    w2_words, w2_scales = pack_weight(0.56 * n((K2, H)) / np.sqrt(K2) / s2, "e4m3")
    w3_words, w3_scales = pack_weight(3.0 * n((K2, H)) / np.sqrt(K2) / s2 * u.T, "e2m1")
    return {
        "tab_words": tab_words, "tab_scales": tab_scales,
        "tab2_words": tab2_words, "tab2_scales": tab2_scales,
        "offs": striped(np.random.permutation(T)[:S]),
        "offs2": striped(np.random.permutation(TB)[:S]),
        "offs3": striped(np.random.permutation(T2)[:S]),
        "offs4": striped(np.random.permutation(T2)[:S]),
        "w1": (1.5 * n((K, H)) / np.sqrt(K) / s).astype(np.float32),
        "g1": (1.4 * np.exp(0.3 * n(H)) * u[:, 0]).astype(np.float32),
        "w2_words": w2_words, "w2_scales": w2_scales,
        "w3_words": w3_words, "w3_scales": w3_scales,
        "wg1": np.exp(0.3 * n((128, S))).astype(np.float32),
        "wg2": np.exp(0.3 * n((128, S))).astype(np.float32),
        "fc": (0.6 * n((H, T2)) * u).astype(np.float32),
        "w4": (n((H, N)) / np.sqrt(H) / u).astype(np.float32),
        "resid": (1.0 + 0.5 * n((N, T2))).astype(np.float32),
    }

def reference(tab_words, tab_scales, tab2_words, tab2_scales, offs, offs2, offs3, offs4, w1, g1,
              w2_words, w2_scales, w3_words, w3_scales, wg1, wg2, fc, w4, resid):
    v = unpack_weight(tab_words, tab_scales, "e4m3")[:, unstriped(offs)]
    v2 = unpack_weight(tab2_words, tab2_scales, "e4m3")[:, unstriped(offs2)]
    h1 = f64(g1)[:, None] * np.tanh(mxq(f64(w1), 0, "e4m3").T @ v)
    ph = unpack_weight(w2_words, w2_scales, "e4m3").T @ v2
    h2 = np.sin(ph) * (unpack_weight(w3_words, w3_scales, "e2m1").T @ v2)
    pa = np.zeros((H, T2))
    pa[:, unstriped(offs3)] = np.tile(f64(wg1), (H // 128, 1)) * h1
    pb = np.zeros((H, T2))
    pb[:, unstriped(offs4)] = np.tile(f64(wg2), (H // 128, 1)) * h2
    z = np.maximum(pa, pb) + f64(fc)
    y = mxq(f64(w4), 0, "e4m3").T @ mxq(z, 0, "e4m3")
    return y * f64(resid)

@@ -1,0 +1,308 @@
+import math
+from contextlib import ExitStack
+
+import concourse.mybir as mybir
+from concourse.masks import make_identity
+
+F32 = mybir.dt.float32
+BF16 = mybir.dt.bfloat16
+I32 = mybir.dt.int32
+U32 = mybir.dt.uint32
+U16 = mybir.dt.uint16
+U8 = mybir.dt.uint8
+FP8X4 = mybir.dt.float8_e4m3fn_x4
+FP4X4 = mybir.dt.float4_e2m1fn_x4
+ACT = mybir.ActivationFunctionType
+ALU = mybir.AluOpType
+
+K, K2, H, N, T, TB, S, T2 = 512, 1024, 512, 768, 2048, 1024, 512, 1024
+FLOPS = 2 * S * H * (K + 2 * K2) + 2 * H * N * T2
+
+P = 128
+PACK = 4
+BANK = 512
+SLICES = H // P
+PASSES2 = K2 // (P * PACK)
+HALVES = T2 // BANK
+ROUNDER = 12582912.0
+
+
+def tile_list_occultation_humidity_score_kernel(
+    tc, tab_words, tab_scales, tab2_words, tab2_scales, offs, offs2, offs3, offs4, w1, g1,
+    w2_words, w2_scales, w3_words, w3_scales, wg1, wg2, fc, w4, resid, out,
+):
+    nc = tc.nc
+    with ExitStack() as ctx:
+        sb = ctx.enter_context(tc.tile_pool(name="sb", bufs=1))
+        ps = ctx.enter_context(tc.psum_pool(name="ps", bufs=1))
+
+        def tile(name, shape, dtype, tag=None):
+            return sb.tile(shape, dtype, name=name, tag=tag or name, align_bytes=64)
+
+        def bank(name, b):
+            return ps.tile([P, BANK], F32, name=name, tag="bank%d" % b)
+
+        def cols(i, width=P):
+            return slice(i * width, (i + 1) * width)
+
+        def round_and_interleave(dst, src):
+            nc.scalar.activation(
+                dst[:].rearrange("p (c j) i -> p c i j", j=4),
+                src.rearrange("p i (c j) -> p c i j", j=4),
+                ACT.Copy,
+            )
+
+        def quantize(codes, scales, src):
+            nc.vector.quantize_mx(out=codes.bitcast(FP8X4), scales=scales, in_=src)
+
+        def add_transposed(dst, src, start, stop):
+            nc.tensor.matmul(dst, lhsT=src, rhs=ident[:], is_transpose=True, start=start, stop=stop)
+
+        tab_s = tile("tab_s", [P, T], U8)
+        tab2_s = tile("tab2_s", [P, TB], U8)
+        w2_s = tile("w2_s", [P, H], U8)
+        w3_s = tile("w3_s", [P, PASSES2, H], U8)
+        v2_s1 = tile("v2_s1", [P, S], U8)
+        nc.vector.memset(tab_s[:].bitcast(I32), 0)
+        nc.vector.memset(tab2_s[:].bitcast(I32), 0)
+        nc.vector.memset(w2_s[:].bitcast(I32), 0)
+        nc.vector.memset(w3_s[:].rearrange("p a c -> p (a c)").bitcast(I32), 0)
+        nc.vector.memset(v2_s1[:].bitcast(I32), 0)
+        page_a = [tile("page_a%d" % t, [P, T2], F32) for t in range(SLICES)]
+        for t in range(SLICES):
+            nc.vector.memset(page_a[t][:], 0.0)
+        ident = tile("ident", [P, P], F32)
+        make_identity(nc, ident[:])
+
+        list1 = tile("list1", [P, S // 16], U16)
+        list2 = tile("list2", [P, S // 16], U16)
+        list3 = tile("list3", [P, S // 16], U16)
+        list4 = tile("list4", [P, S // 16], U16)
+        tab_w = tile("tab_w", [P, T], U32)
+        tab2_w = [tile("tab2_w%d" % a, [P, TB], U32, tag="late%d" % a) for a in range(PASSES2)]
+        w1_raw = [tile("w1_raw0", [P, PACK, H // 2], F32), tile("w1_raw1", [P, PACK, H // 2], F32, tag="late2")]
+        w1_rows = w1.rearrange("(p i) c -> p i c", i=PACK)
+        gain = tile("gain", [P, SLICES], F32)
+        wg1_t = tile("wg1_t", [P, S], F32)
+        wg2_t = tile("wg2_t", [P, S], F32)
+        w2_w = tile("w2_w", [P, PASSES2, H], U32)
+        w3_w = tile("w3_w", [P, PASSES2, 2 * H], U8)
+        fc_t = [tile("fc_t%d" % t, [P, T2], F32) for t in range(SLICES)]
+        w4_raw = tile("w4_raw", [P, PACK, N], F32)
+        res = [tile("res%d" % n, [P, T2], F32) for n in range(N // P)]
+
+        def words(ap):
+            return ap.rearrange("p t i -> p (t i)").bitcast(I32)
+
+        nc.sync.dma_start(list1[:], offs)
+        nc.sync.dma_start(list2[:], offs2)
+        for q in range(4):
+            nc.sync.dma_start(tab_s[32 * q : 32 * q + 4, :].bitcast(I32), tab_scales[0, 4 * q : 4 * q + 4, :].bitcast(I32))
+        nc.sync.dma_start(tab_w[:].bitcast(I32), words(tab_words[0]))
+        nc.sync.dma_start(w1_raw[0][:], w1_rows[:, :, cols(0, H // 2)])
+        nc.sync.dma_start(tab2_w[0][:].bitcast(I32), words(tab2_words[0]))
+        nc.sync.dma_start(wg1_t[:], wg1)
+        for q in range(4):
+            nc.scalar.dma_start(tab2_s[32 * q : 32 * q + 8, :].bitcast(I32), tab2_scales[:, 4 * q : 4 * q + 4, :].bitcast(I32))
+        with nc.allow_non_contiguous_dma(reason="one gain for each partition and slice"):
+            nc.scalar.dma_start(gain[:], g1.rearrange("(t p) -> p t", p=P))
+        nc.sync.dma_start(list3[:], offs3)
+        nc.sync.dma_start(tab2_w[1][:].bitcast(I32), words(tab2_words[1]))
+        nc.sync.dma_start(w1_raw[1][:], w1_rows[:, :, cols(1, H // 2)])
+        for q in range(4):
+            nc.gpsimd.dma_start(w2_s[32 * q : 32 * q + 8, :].bitcast(I32), w2_scales[:, 4 * q : 4 * q + 4, :].bitcast(I32))
+        for q in range(4):
+            nc.gpsimd.dma_start(
+                w3_s[32 * q : 32 * q + 4, :, :].bitcast(I32),
+                w3_scales[:, 4 * q : 4 * q + 4, :].rearrange("a r c -> r a c").bitcast(I32),
+            )
+        nc.sync.dma_start(w2_w[:].bitcast(I32), w2_words.rearrange("a p c i -> p a (c i)").bitcast(I32))
+        nc.sync.dma_start(w3_w[:].bitcast(I32), w3_words.rearrange("a p c -> p a c").bitcast(I32))
+        nc.sync.dma_start(wg2_t[:], wg2)
+        nc.sync.dma_start(list4[:], offs4)
+        for t in range(SLICES):
+            nc.sync.dma_start(fc_t[t][:], fc[cols(t), :])
+        nc.sync.dma_start(w4_raw[:], w4.rearrange("(p i) n -> p i n", i=PACK))
+        for n in range(N // P):
+            nc.sync.dma_start(res[n][:], resid[cols(n), :])
+
+        v_s = tile("v_s", [P, S], U8)
+        v_w = tile("v_w", [P, S], U32)
+        v2_s = tile("v2_s", [P, S], U8)
+        v2_w = [tile("v2_w%d" % a, [P, S], U32) for a in range(PASSES2)]
+        w1_bf = [tile("w1_bf0", [P, H // 2, PACK], BF16), tile("w1_bf1", [P, H // 2, PACK], BF16, tag="late3")]
+        w1_w = [tile("w1_w%d" % h, [P, H // 2], U32) for h in range(2)]
+        w1_s = [tile("w1_s%d" % h, [P, H // 2], U8) for h in range(2)]
+        gained = [tile("gained%d" % t, [P, S], F32) for t in range(SLICES)]
+        tanh = [tile("tanh%d" % t, [P, S], F32) for t in range(SLICES)]
+
+        def quantize_w1(h):
+            round_and_interleave(w1_bf[h], w1_raw[h][:])
+            quantize(w1_w[h][:], w1_s[h][:], w1_bf[h][:].rearrange("p c i -> p (c i)"))
+
+        def bending(t):
+            h, c = divmod(t, 2)
+            acc = bank("h1_%d" % t, t)
+            nc.tensor.matmul_mx(
+                out=acc[:], lhsT=w1_w[h][:, cols(c)].bitcast(FP8X4), lhsT_scale=w1_s[h][:, cols(c)],
+                rhs=v_w[:].bitcast(FP8X4), rhs_scale=v_s[:], start=True, stop=True,
+            )
+            nc.scalar.activation(gained[t][:], wg1_t[:], ACT.Copy, scale=gain[:, t : t + 1])
+            nc.scalar.activation(tanh[t][:], acc[:], ACT.Tanh)
+
+        def place_a(t):
+            nc.vector.tensor_tensor(page_a[t][:].indirect(list3[:]), tanh[t][:], gained[t][:], ALU.mult)
+
+        nc.vector.tensor_copy(v_s[:], tab_s[:].indirect(list1[:]))
+        nc.vector.tensor_copy(v_w[:], tab_w[:].indirect(list1[:]))
+        nc.vector.tensor_copy(v2_s[:], tab2_s[:].indirect(list2[:]))
+        nc.gpsimd.dma_start(v2_s1[0:100, :].bitcast(I32), v2_s[4:104, :].bitcast(I32))
+        quantize_w1(0)
+        bending(0)
+        bending(1)
+        nc.vector.tensor_copy(v2_w[0][:], tab2_w[0][:].indirect(list2[:]))
+        place_a(0)
+        nc.vector.tensor_copy(v2_w[1][:], tab2_w[1][:].indirect(list2[:]))
+        quantize_w1(1)
+        bending(2)
+        bending(3)
+        place_a(1)
+
+        page_b = [tile("page_b%d" % t, [P, T2], F32, tag="late%d" % ((t + 2) % 4)) for t in range(SLICES)]
+        for t in range(SLICES):
+            nc.gpsimd.memset(page_b[t][:], 0.0)
+
+        turns = [tile("turns%d" % j, [P, H], F32) for j in range(S // P)]
+        whole = [tile("whole%d" % j, [P, H], F32) for j in range(S // P)]
+        frac = [bank("frac%d" % t, t) for t in range(SLICES)]
+        for j in range(S // P):
+            acc = bank("phase%d" % j, 4 + j)
+            for a in range(PASSES2):
+                nc.tensor.matmul_mx(
+                    out=acc[:], lhsT=v2_w[a][:, cols(j)].bitcast(FP8X4), lhsT_scale=v2_s[4 * a : P, cols(j)],
+                    rhs=w2_w[:, a, :].bitcast(FP8X4), rhs_scale=w2_s[4 * a : P, :],
+                    start=(a == 0), stop=(a == PASSES2 - 1),
+                )
+            rounded = tile("rounded%d" % j, [P, H], U32, tag="rounded%d" % (j % 2))
+            nc.scalar.activation(rounded[:], acc[:], ACT.Copy, scale=0.5 / math.pi, bias=ROUNDER)
+            nc.scalar.activation(turns[j][:], acc[:], ACT.Copy, scale=0.5 / math.pi)
+            nc.scalar.activation(whole[j][:], rounded[:], ACT.Copy, scale=-1.0, bias=ROUNDER)
+            for t in range(SLICES):
+                add_transposed(frac[t][:, cols(j)], turns[j][:, cols(t)], j == 0, False)
+                add_transposed(frac[t][:, cols(j)], whole[j][:, cols(t)], False, j == S // P - 1)
+        place_a(2)
+        place_a(3)
+
+        sine = [tile("sine%d" % t, [P, S], F32) for t in range(SLICES)]
+        weighted = [tile("weighted%d" % t, [P, S], F32) for t in range(SLICES)]
+        for t in range(SLICES):
+            nc.scalar.activation(sine[t][:], frac[t][:], ACT.Sin, scale=2.0 * math.pi)
+
+        def surface(t):
+            acc = bank("h3_%d" % t, 4 + t)
+            for a in range(PASSES2):
+                nc.tensor.matmul_mx(
+                    out=acc[:], lhsT=w3_w[:, a, cols(t, 2 * P)].bitcast(FP4X4), lhsT_scale=w3_s[:, a, cols(t)],
+                    rhs=v2_w[a][:].bitcast(FP8X4), rhs_scale=(v2_s, v2_s1)[a][:],
+                    start=(a == 0), stop=(a == PASSES2 - 1),
+                )
+            nc.vector.tensor_tensor(weighted[t][:], acc[:], wg2_t[:], ALU.mult)
+
+        def place_b(t):
+            nc.vector.tensor_tensor(page_b[t][:].indirect(list4[:]), sine[t][:], weighted[t][:], ALU.mult)
+
+        def word_order(ap):
+            return ap.rearrange("p (b q u e) -> p u b q e", b=4, u=2, e=2)
+
+        def turned_sum(name, b, page, t, h):
+            acc = bank(name, b)
+            for i in range(4):
+                add_transposed(acc[:, cols(i)], fc_t[t][:, cols(4 * h + i)], i == 0, False)
+            for i in range(4):
+                add_transposed(acc[:, cols(i)], page[:, cols(4 * h + i)], False, i == 3)
+            return acc
+
+        side_a = {}
+        z_turned = [tile("z_turned%d" % h, [P, 4 * H], BF16) for h in range(HALVES)]
+
+        def turn_a(t):
+            for h in range(HALVES):
+                acc = turned_sum("sum_a%d_%d" % (t, h), 2 * (t % 2) + h, page_a[t], t, h)
+                side_a[t, h] = tile("side_a%d_%d" % (t, h), [P, BANK], F32)
+                nc.scalar.copy(side_a[t, h][:].rearrange("p (u b q e) -> p u b q e", u=2, b=4, e=2), word_order(acc[:]))
+
+        side_b = {}
+
+        def turn_b(t):
+            for h in range(HALVES):
+                side_b[t, h] = turned_sum("sum_b%d_%d" % (t, h), 4 + 2 * (t % 2) + h, page_b[t], t, h)
+
+        def larger(t, h):
+            nc.vector.tensor_tensor(
+                z_turned[h][:].rearrange("p (b u q e) -> p u b q e", b=4, u=2, e=2)[:, :, :, cols(t, 32), :],
+                word_order(side_b[t, h][:]),
+                side_a[t, h][:].rearrange("p (u b q e) -> p u b q e", u=2, b=4, e=2),
+                ALU.max,
+            )
+
+        w4_bf = [tile("w4_bf%d" % h, [P, N // 2, PACK], BF16) for h in range(2)]
+        w4_w = tile("w4_w", [P, N], U32)
+        w4_s = tile("w4_s", [P, N], U8)
+
+        surface(0)
+        surface(1)
+        place_b(0)
+        for t in range(SLICES):
+            turn_a(t)
+        surface(2)
+        surface(3)
+        turn_b(0)
+        place_b(1)
+        for h in range(2):
+            round_and_interleave(w4_bf[h], w4_raw[:, :, cols(h, N // 2)])
+        turn_b(1)
+        larger(0, 0)
+        larger(0, 1)
+        place_b(2)
+        turn_b(2)
+        larger(1, 0)
+        larger(1, 1)
+        for h in range(2):
+            quantize(w4_w[:, cols(h, N // 2)], w4_s[:, cols(h, N // 2)], w4_bf[h][:].rearrange("p c i -> p (c i)"))
+        place_b(3)
+        turn_b(3)
+
+        z_w = [tile("z_w%d" % h, [P, BANK], U32) for h in range(HALVES)]
+        z_s = [tile("z_s%d" % h, [P, BANK], U8) for h in range(HALVES)]
+        z_in = {}
+
+        def turn_back(h):
+            pairs = z_turned[h][:].bitcast(F32)
+            for c in range(2):
+                acc = bank("z_pairs%d_%d" % (h, c), 2 * h + c)
+                for i in range(4):
+                    nc.tensor.transpose(acc[:, cols(i)], pairs[:, cols(4 * c + i)], ident[:])
+                z_in[h, c] = tile("z_in%d_%d" % (h, c), [P, BANK * 2], BF16)
+                nc.scalar.copy(
+                    z_in[h, c][:].bitcast(F32).rearrange("p (b m u) -> p b m u", b=2, u=2),
+                    acc[:].rearrange("p (b u m) -> p b m u", b=2, u=2),
+                )
+
+        def score(h):
+            for c in range(2):
+                quantize(z_w[h][:, cols(c, BANK // 2)], z_s[h][:, cols(c, BANK // 2)], z_in[h, c][:])
+            for n in range(N // P):
+                acc = bank("y%d_%d" % (h, n), 4 + (0, 2, 1, 3)[(h * (N // P) + n) % 4])
+                nc.tensor.matmul_mx(
+                    out=acc[:], lhsT=w4_w[:, cols(n)].bitcast(FP8X4), lhsT_scale=w4_s[:, cols(n)],
+                    rhs=z_w[h][:].bitcast(FP8X4), rhs_scale=z_s[h][:], start=True, stop=True,
+                )
+                nc.vector.tensor_tensor(res[n][:, cols(h, BANK)], acc[:], res[n][:, cols(h, BANK)], ALU.mult)
+                nc.sync.dma_start(out[cols(n), cols(h, BANK)], res[n][:, cols(h, BANK)])
+
+        for h in range(HALVES):
+            larger(2, h)
+            larger(3, h)
+            turn_back(h)
+        for h in range(HALVES):
+            score(h)

@@ -23,7 +23,7 @@ PACK = 4
 BANK = 512
 SLICES = H // P
 PASSES2 = K2 // (P * PACK)
-HALVES = T2 // BANK
+QUARTER = T2 // 4
 ROUNDER = 12582912.0
 
 
@@ -63,24 +63,21 @@ def tile_list_occultation_humidity_score_kernel(
         w2_s = tile("w2_s", [P, H], U8)
         w3_s = tile("w3_s", [P, PASSES2, H], U8)
         v2_s1 = tile("v2_s1", [P, S], U8)
-        nc.vector.memset(tab_s[:].bitcast(I32), 0)
-        nc.vector.memset(tab2_s[:].bitcast(I32), 0)
+        nc.gpsimd.memset(tab2_s[:].bitcast(I32), 0)
         nc.vector.memset(w2_s[:].bitcast(I32), 0)
         nc.vector.memset(w3_s[:].rearrange("p a c -> p (a c)").bitcast(I32), 0)
         nc.vector.memset(v2_s1[:].bitcast(I32), 0)
-        page_a = [tile("page_a%d" % t, [P, T2], F32) for t in range(SLICES)]
-        for t in range(SLICES):
+        page_a = [tile("page_a%d" % t, [P, T2], F32) for t in range(2)]
+        for t in range(2):
             nc.vector.memset(page_a[t][:], 0.0)
-        ident = tile("ident", [P, P], F32)
-        make_identity(nc, ident[:])
 
         list1 = tile("list1", [P, S // 16], U16)
         list2 = tile("list2", [P, S // 16], U16)
         list3 = tile("list3", [P, S // 16], U16)
         list4 = tile("list4", [P, S // 16], U16)
         tab_w = tile("tab_w", [P, T], U32)
-        tab2_w = [tile("tab2_w%d" % a, [P, TB], U32, tag="late%d" % a) for a in range(PASSES2)]
-        w1_raw = [tile("w1_raw0", [P, PACK, H // 2], F32), tile("w1_raw1", [P, PACK, H // 2], F32, tag="late2")]
+        tab2_w = [tile("tab2_w%d" % a, [P, TB], U32) for a in range(PASSES2)]
+        w1_raw = [tile("w1_raw%d" % h, [P, PACK, H // 2], F32) for h in range(2)]
         w1_rows = w1.rearrange("(p i) c -> p i c", i=PACK)
         gain = tile("gain", [P, SLICES], F32)
         wg1_t = tile("wg1_t", [P, S], F32)
@@ -89,48 +86,54 @@ def tile_list_occultation_humidity_score_kernel(
         w3_w = tile("w3_w", [P, PASSES2, 2 * H], U8)
         fc_t = [tile("fc_t%d" % t, [P, T2], F32) for t in range(SLICES)]
         w4_raw = tile("w4_raw", [P, PACK, N], F32)
-        res = [tile("res%d" % n, [P, T2], F32) for n in range(N // P)]
+        res = [tile("res%d" % n, [P, 2, T2], F32) for n in range(N // (2 * P))]
 
         def words(ap):
             return ap.rearrange("p t i -> p (t i)").bitcast(I32)
 
+        def row_pair(ap, n):
+            return ap[cols(n, 2 * P), :].rearrange("(i p) m -> p i m", p=P)
+
         nc.sync.dma_start(list1[:], offs)
-        nc.sync.dma_start(list2[:], offs2)
         for q in range(4):
-            nc.sync.dma_start(tab_s[32 * q : 32 * q + 4, :].bitcast(I32), tab_scales[0, 4 * q : 4 * q + 4, :].bitcast(I32))
+            rows = tab_scales[0, 4 * q : 4 * q + 4, :].bitcast(I32)
+            nc.sync.dma_start(tab_s[32 * q : 32 * q + 32, :].bitcast(I32), rows.unsqueeze(0).broadcast_to([8, 4, T // 4]))
         nc.sync.dma_start(tab_w[:].bitcast(I32), words(tab_words[0]))
+        nc.sync.dma_start(list2[:], offs2)
         nc.sync.dma_start(w1_raw[0][:], w1_rows[:, :, cols(0, H // 2)])
-        nc.sync.dma_start(tab2_w[0][:].bitcast(I32), words(tab2_words[0]))
-        nc.sync.dma_start(wg1_t[:], wg1)
         for q in range(4):
-            nc.scalar.dma_start(tab2_s[32 * q : 32 * q + 8, :].bitcast(I32), tab2_scales[:, 4 * q : 4 * q + 4, :].bitcast(I32))
+            nc.sync.dma_start(tab2_s[32 * q : 32 * q + 8, :].bitcast(I32), tab2_scales[:, 4 * q : 4 * q + 4, :].bitcast(I32))
+        nc.sync.dma_start(w1_raw[1][:], w1_rows[:, :, cols(1, H // 2)])
         with nc.allow_non_contiguous_dma(reason="one gain for each partition and slice"):
-            nc.scalar.dma_start(gain[:], g1.rearrange("(t p) -> p t", p=P))
+            nc.sync.dma_start(gain[:], g1.rearrange("(t p) -> p t", p=P))
+        nc.sync.dma_start(wg1_t[:], wg1)
+        nc.sync.dma_start(tab2_w[0][:].bitcast(I32), words(tab2_words[0]))
         nc.sync.dma_start(list3[:], offs3)
         nc.sync.dma_start(tab2_w[1][:].bitcast(I32), words(tab2_words[1]))
-        nc.sync.dma_start(w1_raw[1][:], w1_rows[:, :, cols(1, H // 2)])
-        for q in range(4):
-            nc.gpsimd.dma_start(w2_s[32 * q : 32 * q + 8, :].bitcast(I32), w2_scales[:, 4 * q : 4 * q + 4, :].bitcast(I32))
-        for q in range(4):
-            nc.gpsimd.dma_start(
-                w3_s[32 * q : 32 * q + 4, :, :].bitcast(I32),
-                w3_scales[:, 4 * q : 4 * q + 4, :].rearrange("a r c -> r a c").bitcast(I32),
-            )
         nc.sync.dma_start(w2_w[:].bitcast(I32), w2_words.rearrange("a p c i -> p a (c i)").bitcast(I32))
+        for q in range(4):
+            nc.sync.dma_start(w2_s[32 * q : 32 * q + 8, :].bitcast(I32), w2_scales[:, 4 * q : 4 * q + 4, :].bitcast(I32))
         nc.sync.dma_start(w3_w[:].bitcast(I32), w3_words.rearrange("a p c -> p a c").bitcast(I32))
         nc.sync.dma_start(wg2_t[:], wg2)
         nc.sync.dma_start(list4[:], offs4)
+        for q in range(4):
+            nc.sync.dma_start(
+                w3_s[32 * q : 32 * q + 4, :, :].bitcast(I32),
+                w3_scales[:, 4 * q : 4 * q + 4, :].rearrange("a r c -> r a c").bitcast(I32),
+            )
+        nc.sync.dma_start(w4_raw[:], w4.rearrange("(p i) n -> p i n", i=PACK))
         for t in range(SLICES):
             nc.sync.dma_start(fc_t[t][:], fc[cols(t), :])
-        nc.sync.dma_start(w4_raw[:], w4.rearrange("(p i) n -> p i n", i=PACK))
-        for n in range(N // P):
-            nc.sync.dma_start(res[n][:], resid[cols(n), :])
+        for n in range(N // (2 * P)):
+            nc.sync.dma_start(res[n][:], row_pair(resid, n))
+        ident = tile("ident", [P, P], F32)
+        make_identity(nc, ident[:])
 
         v_s = tile("v_s", [P, S], U8)
         v_w = tile("v_w", [P, S], U32)
         v2_s = tile("v2_s", [P, S], U8)
         v2_w = [tile("v2_w%d" % a, [P, S], U32) for a in range(PASSES2)]
-        w1_bf = [tile("w1_bf0", [P, H // 2, PACK], BF16), tile("w1_bf1", [P, H // 2, PACK], BF16, tag="late3")]
+        w1_bf = [tile("w1_bf%d" % h, [P, H // 2, PACK], BF16) for h in range(2)]
         w1_w = [tile("w1_w%d" % h, [P, H // 2], U32) for h in range(2)]
         w1_s = [tile("w1_s%d" % h, [P, H // 2], U8) for h in range(2)]
         gained = [tile("gained%d" % t, [P, S], F32) for t in range(SLICES)]
@@ -153,52 +156,62 @@ def tile_list_occultation_humidity_score_kernel(
         def place_a(t):
             nc.vector.tensor_tensor(page_a[t][:].indirect(list3[:]), tanh[t][:], gained[t][:], ALU.mult)
 
+        def cleared_page(name, tag):
+            page = tile(name, [P, T2], F32, tag=tag)
+            nc.gpsimd.memset(page[:], 0.0)
+            return page
+
         nc.vector.tensor_copy(v_s[:], tab_s[:].indirect(list1[:]))
         nc.vector.tensor_copy(v_w[:], tab_w[:].indirect(list1[:]))
         nc.vector.tensor_copy(v2_s[:], tab2_s[:].indirect(list2[:]))
         nc.gpsimd.dma_start(v2_s1[0:100, :].bitcast(I32), v2_s[4:104, :].bitcast(I32))
         quantize_w1(0)
+        quantize_w1(1)
+        nc.vector.tensor_copy(v2_w[0][:], tab2_w[0][:].indirect(list2[:]))
+        nc.vector.tensor_copy(v2_w[1][:], tab2_w[1][:].indirect(list2[:]))
         bending(0)
         bending(1)
-        nc.vector.tensor_copy(v2_w[0][:], tab2_w[0][:].indirect(list2[:]))
-        place_a(0)
-        nc.vector.tensor_copy(v2_w[1][:], tab2_w[1][:].indirect(list2[:]))
-        quantize_w1(1)
         bending(2)
         bending(3)
+        place_a(0)
+        page_a.append(cleared_page("page_a2", "gained0"))
+        page_a.append(cleared_page("page_a3", "tanh0"))
+        page_b = [cleared_page("page_b0", "tab2_w1")]
         place_a(1)
-
-        page_b = [tile("page_b%d" % t, [P, T2], F32, tag="late%d" % ((t + 2) % 4)) for t in range(SLICES)]
-        for t in range(SLICES):
-            nc.gpsimd.memset(page_b[t][:], 0.0)
+        page_b.append(cleared_page("page_b1", "gained1"))
+        page_b.append(cleared_page("page_b2", "tanh1"))
 
         turns = [tile("turns%d" % j, [P, H], F32) for j in range(S // P)]
         whole = [tile("whole%d" % j, [P, H], F32) for j in range(S // P)]
         frac = [bank("frac%d" % t, t) for t in range(SLICES)]
+        phase = [bank("phase%d" % j, 4 + j) for j in range(S // P)]
         for j in range(S // P):
-            acc = bank("phase%d" % j, 4 + j)
             for a in range(PASSES2):
                 nc.tensor.matmul_mx(
-                    out=acc[:], lhsT=v2_w[a][:, cols(j)].bitcast(FP8X4), lhsT_scale=v2_s[4 * a : P, cols(j)],
+                    out=phase[j][:], lhsT=v2_w[a][:, cols(j)].bitcast(FP8X4), lhsT_scale=v2_s[4 * a : P, cols(j)],
                     rhs=w2_w[:, a, :].bitcast(FP8X4), rhs_scale=w2_s[4 * a : P, :],
                     start=(a == 0), stop=(a == PASSES2 - 1),
                 )
+        for j in range(S // P):
             rounded = tile("rounded%d" % j, [P, H], U32, tag="rounded%d" % (j % 2))
-            nc.scalar.activation(rounded[:], acc[:], ACT.Copy, scale=0.5 / math.pi, bias=ROUNDER)
-            nc.scalar.activation(turns[j][:], acc[:], ACT.Copy, scale=0.5 / math.pi)
+            nc.scalar.activation(rounded[:], phase[j][:], ACT.Copy, scale=0.5 / math.pi, bias=ROUNDER)
+            nc.scalar.activation(turns[j][:], phase[j][:], ACT.Copy, scale=0.5 / math.pi)
             nc.scalar.activation(whole[j][:], rounded[:], ACT.Copy, scale=-1.0, bias=ROUNDER)
             for t in range(SLICES):
                 add_transposed(frac[t][:, cols(j)], turns[j][:, cols(t)], j == 0, False)
+            for t in range(SLICES):
                 add_transposed(frac[t][:, cols(j)], whole[j][:, cols(t)], False, j == S // P - 1)
         place_a(2)
+        page_b.append(cleared_page("page_b3", "gained2"))
         place_a(3)
 
         sine = [tile("sine%d" % t, [P, S], F32) for t in range(SLICES)]
-        weighted = [tile("weighted%d" % t, [P, S], F32) for t in range(SLICES)]
         for t in range(SLICES):
             nc.scalar.activation(sine[t][:], frac[t][:], ACT.Sin, scale=2.0 * math.pi)
 
-        def surface(t):
+        weighted = {}
+
+        def surface(t, tag):
             acc = bank("h3_%d" % t, 4 + t)
             for a in range(PASSES2):
                 nc.tensor.matmul_mx(
@@ -206,103 +219,100 @@ def tile_list_occultation_humidity_score_kernel(
                     rhs=v2_w[a][:].bitcast(FP8X4), rhs_scale=(v2_s, v2_s1)[a][:],
                     start=(a == 0), stop=(a == PASSES2 - 1),
                 )
+            weighted[t] = tile("weighted%d" % t, [P, S], F32, tag=tag)
             nc.vector.tensor_tensor(weighted[t][:], acc[:], wg2_t[:], ALU.mult)
 
         def place_b(t):
             nc.vector.tensor_tensor(page_b[t][:].indirect(list4[:]), sine[t][:], weighted[t][:], ALU.mult)
 
-        def word_order(ap):
-            return ap.rearrange("p (b q u e) -> p u b q e", b=4, u=2, e=2)
+        z_turned = [tile("z_turned%d" % c, [P, 2 * H], BF16) for c in range(4)]
+        sums = {}
 
-        def turned_sum(name, b, page, t, h):
-            acc = bank(name, b)
-            for i in range(4):
-                add_transposed(acc[:, cols(i)], fc_t[t][:, cols(4 * h + i)], i == 0, False)
-            for i in range(4):
-                add_transposed(acc[:, cols(i)], page[:, cols(4 * h + i)], False, i == 3)
-            return acc
+        def open_sum(t, c0, c1, b):
+            sums[t, c0] = bank("sum%d_%d" % (t, c0), b)
+            for i in range(2 * (c1 - c0)):
+                add_transposed(sums[t, c0][:, cols(i)], fc_t[t][:, cols(2 * c0 + i)], i == 0, False)
 
-        side_a = {}
-        z_turned = [tile("z_turned%d" % h, [P, 4 * H], BF16) for h in range(HALVES)]
+        def larger(t, c0, c1, tag=None):
+            levels = slice(c0 * QUARTER, c1 * QUARTER)
+            top = tile("top%d_%d" % (t, c0), [P, (c1 - c0) * QUARTER], F32, tag=tag)
+            nc.vector.tensor_tensor(top[:], page_a[t][:, levels], page_b[t][:, levels], ALU.max)
+            for i in range(2 * (c1 - c0)):
+                add_transposed(sums[t, c0][:, cols(i)], top[:, cols(i)], False, i == 2 * (c1 - c0) - 1)
+            for c in range(c0, c1):
+                nc.scalar.copy(
+                    z_turned[c][:].rearrange("p (b u q e) -> p u b q e", b=2, u=2, e=2)[:, :, :, cols(t, 32), :],
+                    sums[t, c0][:, cols(c - c0, QUARTER)].rearrange("p (b q u e) -> p u b q e", b=2, u=2, e=2),
+                )
 
-        def turn_a(t):
-            for h in range(HALVES):
-                acc = turned_sum("sum_a%d_%d" % (t, h), 2 * (t % 2) + h, page_a[t], t, h)
-                side_a[t, h] = tile("side_a%d_%d" % (t, h), [P, BANK], F32)
-                nc.scalar.copy(side_a[t, h][:].rearrange("p (u b q e) -> p u b q e", u=2, b=4, e=2), word_order(acc[:]))
-
-        side_b = {}
-
-        def turn_b(t):
-            for h in range(HALVES):
-                side_b[t, h] = turned_sum("sum_b%d_%d" % (t, h), 4 + 2 * (t % 2) + h, page_b[t], t, h)
-
-        def larger(t, h):
-            nc.vector.tensor_tensor(
-                z_turned[h][:].rearrange("p (b u q e) -> p u b q e", b=4, u=2, e=2)[:, :, :, cols(t, 32), :],
-                word_order(side_b[t, h][:]),
-                side_a[t, h][:].rearrange("p (u b q e) -> p u b q e", u=2, b=4, e=2),
-                ALU.max,
-            )
-
-        w4_bf = [tile("w4_bf%d" % h, [P, N // 2, PACK], BF16) for h in range(2)]
         w4_w = tile("w4_w", [P, N], U32)
         w4_s = tile("w4_s", [P, N], U8)
 
-        surface(0)
-        surface(1)
+        w4_bf = [tile("w4_bf%d" % i, [P, N // 3, PACK], BF16) for i in range(3)]
+        for i in range(3):
+            round_and_interleave(w4_bf[i], w4_raw[:, :, cols(i, N // 3)])
+        for t in range(SLICES - 1):
+            surface(t, None)
         place_b(0)
-        for t in range(SLICES):
-            turn_a(t)
-        surface(2)
-        surface(3)
-        turn_b(0)
         place_b(1)
-        for h in range(2):
-            round_and_interleave(w4_bf[h], w4_raw[:, :, cols(h, N // 2)])
-        turn_b(1)
-        larger(0, 0)
-        larger(0, 1)
+        open_sum(0, 0, 2, 0)
+        larger(0, 0, 2, "sine1")
         place_b(2)
-        turn_b(2)
-        larger(1, 0)
-        larger(1, 1)
-        for h in range(2):
-            quantize(w4_w[:, cols(h, N // 2)], w4_s[:, cols(h, N // 2)], w4_bf[h][:].rearrange("p c i -> p (c i)"))
+        for i in range(3):
+            quantize(w4_w[:, cols(i, N // 3)], w4_s[:, cols(i, N // 3)], w4_bf[i][:].rearrange("p c i -> p (c i)"))
+        surface(3, "w4_bf2")
+        open_sum(1, 0, 2, 1)
+        larger(1, 0, 2, "wg2_t")
+        open_sum(2, 0, 2, 0)
+        open_sum(3, 0, 1, 2)
+        open_sum(3, 1, 2, 3)
+        for t in range(SLICES):
+            open_sum(t, 2, 4, 4 + t)
         place_b(3)
-        turn_b(3)
 
-        z_w = [tile("z_w%d" % h, [P, BANK], U32) for h in range(HALVES)]
-        z_s = [tile("z_s%d" % h, [P, BANK], U8) for h in range(HALVES)]
+        z_w = [tile("z_w%d" % c, [P, QUARTER], U32) for c in range(4)]
+        z_s = [tile("z_s%d" % c, [P, QUARTER], U8) for c in range(4)]
         z_in = {}
 
-        def turn_back(h):
-            pairs = z_turned[h][:].bitcast(F32)
-            for c in range(2):
-                acc = bank("z_pairs%d_%d" % (h, c), 2 * h + c)
-                for i in range(4):
-                    nc.tensor.transpose(acc[:, cols(i)], pairs[:, cols(4 * c + i)], ident[:])
-                z_in[h, c] = tile("z_in%d_%d" % (h, c), [P, BANK * 2], BF16)
-                nc.scalar.copy(
-                    z_in[h, c][:].bitcast(F32).rearrange("p (b m u) -> p b m u", b=2, u=2),
-                    acc[:].rearrange("p (b u m) -> p b m u", b=2, u=2),
-                )
+        def turn_back(c, b):
+            pairs = z_turned[c][:].bitcast(F32)
+            acc = bank("z_pairs%d" % c, b)
+            for i in range(4):
+                nc.tensor.transpose(acc[:, cols(i)], pairs[:, cols(i)], ident[:])
+            z_in[c] = tile("z_in%d" % c, [P, QUARTER * PACK], BF16)
+            nc.scalar.copy(
+                z_in[c][:].bitcast(F32).rearrange("p (b m u) -> p b m u", b=2, u=2),
+                acc[:].rearrange("p (b u m) -> p b m u", b=2, u=2),
+            )
 
-        def score(h):
-            for c in range(2):
-                quantize(z_w[h][:, cols(c, BANK // 2)], z_s[h][:, cols(c, BANK // 2)], z_in[h, c][:])
-            for n in range(N // P):
-                acc = bank("y%d_%d" % (h, n), 4 + (0, 2, 1, 3)[(h * (N // P) + n) % 4])
-                nc.tensor.matmul_mx(
-                    out=acc[:], lhsT=w4_w[:, cols(n)].bitcast(FP8X4), lhsT_scale=w4_s[:, cols(n)],
-                    rhs=z_w[h][:].bitcast(FP8X4), rhs_scale=z_s[h][:], start=True, stop=True,
-                )
-                nc.vector.tensor_tensor(res[n][:, cols(h, BANK)], acc[:], res[n][:, cols(h, BANK)], ALU.mult)
-                nc.sync.dma_start(out[cols(n), cols(h, BANK)], res[n][:, cols(h, BANK)])
+        score_banks = (2, 3, 1, 0, 6, 7, 2, 3, 1, 0, 4, 5)
 
-        for h in range(HALVES):
-            larger(2, h)
-            larger(3, h)
-            turn_back(h)
-        for h in range(HALVES):
-            score(h)
+        def score(c):
+            for n in range(N // (2 * P)):
+                acc = bank("y%d_%d" % (c, n), score_banks[3 * c + n])
+                for i in range(2):
+                    nc.tensor.matmul_mx(
+                        out=acc[:, cols(i, QUARTER)], lhsT=w4_w[:, cols(2 * n + i)].bitcast(FP8X4),
+                        lhsT_scale=w4_s[:, cols(2 * n + i)],
+                        rhs=z_w[c][:].bitcast(FP8X4), rhs_scale=z_s[c][:], start=True, stop=True,
+                    )
+                part = res[n][:, :, cols(c, QUARTER)]
+                nc.vector.tensor_tensor(part, acc[:].rearrange("p (i m) -> p i m", i=2), part, ALU.mult)
+                nc.sync.dma_start(row_pair(out, n)[:, :, cols(c, QUARTER)], part)
+
+        larger(2, 0, 2, "sine3")
+        larger(3, 0, 1)
+        turn_back(0, 1)
+        larger(3, 1, 2)
+        turn_back(1, 0)
+        larger(0, 2, 4, "w4_bf2")
+        larger(1, 2, 4, "sine3")
+        larger(2, 2, 4, "top3_0")
+        larger(3, 2, 4)
+        turn_back(2, 4)
+        turn_back(3, 5)
+        quantize(z_w[0][:], z_s[0][:], z_in[0][:])
+        for c in range(4):
+            if c + 1 < 4:
+                quantize(z_w[c + 1][:], z_s[c + 1][:], z_in[c + 1][:])
+            score(c)

@@ -47,7 +47,7 @@ def tile_list_occultation_humidity_score_kernel(
 
         def round_and_interleave(dst, src):
             nc.scalar.activation(
-                dst[:].rearrange("p (c j) i -> p c i j", j=4),
+                dst.rearrange("p (c j) i -> p c i j", j=4),
                 src.rearrange("p i (c j) -> p c i j", j=4),
                 ACT.Copy,
             )
@@ -63,13 +63,10 @@ def tile_list_occultation_humidity_score_kernel(
         w2_s = tile("w2_s", [P, H], U8)
         w3_s = tile("w3_s", [P, PASSES2, H], U8)
         v2_s1 = tile("v2_s1", [P, S], U8)
-        nc.gpsimd.memset(tab2_s[:].bitcast(I32), 0)
+        nc.vector.memset(tab2_s[:].bitcast(I32), 0)
         nc.vector.memset(w2_s[:].bitcast(I32), 0)
         nc.vector.memset(w3_s[:].rearrange("p a c -> p (a c)").bitcast(I32), 0)
         nc.vector.memset(v2_s1[:].bitcast(I32), 0)
-        page_a = [tile("page_a%d" % t, [P, T2], F32) for t in range(2)]
-        for t in range(2):
-            nc.vector.memset(page_a[t][:], 0.0)
 
         list1 = tile("list1", [P, S // 16], U16)
         list2 = tile("list2", [P, S // 16], U16)
@@ -113,19 +110,6 @@ def tile_list_occultation_humidity_score_kernel(
         nc.sync.dma_start(w2_w[:].bitcast(I32), w2_words.rearrange("a p c i -> p a (c i)").bitcast(I32))
         for q in range(4):
             nc.sync.dma_start(w2_s[32 * q : 32 * q + 8, :].bitcast(I32), w2_scales[:, 4 * q : 4 * q + 4, :].bitcast(I32))
-        nc.sync.dma_start(w3_w[:].bitcast(I32), w3_words.rearrange("a p c -> p a c").bitcast(I32))
-        nc.sync.dma_start(wg2_t[:], wg2)
-        nc.sync.dma_start(list4[:], offs4)
-        for q in range(4):
-            nc.sync.dma_start(
-                w3_s[32 * q : 32 * q + 4, :, :].bitcast(I32),
-                w3_scales[:, 4 * q : 4 * q + 4, :].rearrange("a r c -> r a c").bitcast(I32),
-            )
-        nc.sync.dma_start(w4_raw[:], w4.rearrange("(p i) n -> p i n", i=PACK))
-        for t in range(SLICES):
-            nc.sync.dma_start(fc_t[t][:], fc[cols(t), :])
-        for n in range(N // (2 * P)):
-            nc.sync.dma_start(res[n][:], row_pair(resid, n))
         ident = tile("ident", [P, P], F32)
         make_identity(nc, ident[:])
 
@@ -140,7 +124,7 @@ def tile_list_occultation_humidity_score_kernel(
         tanh = [tile("tanh%d" % t, [P, S], F32) for t in range(SLICES)]
 
         def quantize_w1(h):
-            round_and_interleave(w1_bf[h], w1_raw[h][:])
+            round_and_interleave(w1_bf[h][:], w1_raw[h][:])
             quantize(w1_w[h][:], w1_s[h][:], w1_bf[h][:].rearrange("p c i -> p (c i)"))
 
         def bending(t):
@@ -156,30 +140,35 @@ def tile_list_occultation_humidity_score_kernel(
         def place_a(t):
             nc.vector.tensor_tensor(page_a[t][:].indirect(list3[:]), tanh[t][:], gained[t][:], ALU.mult)
 
-        def cleared_page(name, tag):
-            page = tile(name, [P, T2], F32, tag=tag)
-            nc.gpsimd.memset(page[:], 0.0)
-            return page
-
         nc.vector.tensor_copy(v_s[:], tab_s[:].indirect(list1[:]))
         nc.vector.tensor_copy(v_w[:], tab_w[:].indirect(list1[:]))
         nc.vector.tensor_copy(v2_s[:], tab2_s[:].indirect(list2[:]))
-        nc.gpsimd.dma_start(v2_s1[0:100, :].bitcast(I32), v2_s[4:104, :].bitcast(I32))
+        nc.sync.dma_start(w3_w[:].bitcast(I32), w3_words.rearrange("a p c -> p a c").bitcast(I32))
+        nc.sync.dma_start(wg2_t[:], wg2)
+        nc.sync.dma_start(list4[:], offs4)
+        for q in range(4):
+            nc.sync.dma_start(
+                w3_s[32 * q : 32 * q + 4, :, :].bitcast(I32),
+                w3_scales[:, 4 * q : 4 * q + 4, :].rearrange("a r c -> r a c").bitcast(I32),
+            )
+        nc.sync.dma_start(v2_s1[0:100, :].bitcast(I32), v2_s[4:104, :].bitcast(I32))
+        nc.sync.dma_start(w4_raw[:], w4.rearrange("(p i) n -> p i n", i=PACK))
+        for t in range(SLICES):
+            nc.sync.dma_start(fc_t[t][:], fc[cols(t), :])
+        for n in range(N // (2 * P)):
+            nc.sync.dma_start(res[n][:], row_pair(resid, n))
         quantize_w1(0)
         quantize_w1(1)
         nc.vector.tensor_copy(v2_w[0][:], tab2_w[0][:].indirect(list2[:]))
         nc.vector.tensor_copy(v2_w[1][:], tab2_w[1][:].indirect(list2[:]))
-        bending(0)
-        bending(1)
-        bending(2)
-        bending(3)
+        page_a = [tile("page_a%d" % t, [P, T2], F32) for t in range(SLICES)]
+        page_b = [tile("page_b%d" % t, [P, T2], F32) for t in range(SLICES)]
+        for page in page_a + page_b:
+            nc.vector.memset(page[:].bitcast(I32), 0)
+        for t in range(SLICES):
+            bending(t)
         place_a(0)
-        page_a.append(cleared_page("page_a2", "gained0"))
-        page_a.append(cleared_page("page_a3", "tanh0"))
-        page_b = [cleared_page("page_b0", "tab2_w1")]
         place_a(1)
-        page_b.append(cleared_page("page_b1", "gained1"))
-        page_b.append(cleared_page("page_b2", "tanh1"))
 
         turns = [tile("turns%d" % j, [P, H], F32) for j in range(S // P)]
         whole = [tile("whole%d" % j, [P, H], F32) for j in range(S // P)]
@@ -202,7 +191,6 @@ def tile_list_occultation_humidity_score_kernel(
             for t in range(SLICES):
                 add_transposed(frac[t][:, cols(j)], whole[j][:, cols(t)], False, j == S // P - 1)
         place_a(2)
-        page_b.append(cleared_page("page_b3", "gained2"))
         place_a(3)
 
         sine = [tile("sine%d" % t, [P, S], F32) for t in range(SLICES)]
@@ -225,7 +213,7 @@ def tile_list_occultation_humidity_score_kernel(
         def place_b(t):
             nc.vector.tensor_tensor(page_b[t][:].indirect(list4[:]), sine[t][:], weighted[t][:], ALU.mult)
 
-        z_turned = [tile("z_turned%d" % c, [P, 2 * H], BF16) for c in range(4)]
+        z_turned = {(c0, c1): tile("z_turned%d" % c0, [P, (c1 - c0) * 2 * H], BF16) for c0, c1 in ((0, 1), (1, 2), (2, 4))}
         sums = {}
 
         def open_sum(t, c0, c1, b):
@@ -239,18 +227,21 @@ def tile_list_occultation_humidity_score_kernel(
             nc.vector.tensor_tensor(top[:], page_a[t][:, levels], page_b[t][:, levels], ALU.max)
             for i in range(2 * (c1 - c0)):
                 add_transposed(sums[t, c0][:, cols(i)], top[:, cols(i)], False, i == 2 * (c1 - c0) - 1)
-            for c in range(c0, c1):
-                nc.scalar.copy(
-                    z_turned[c][:].rearrange("p (b u q e) -> p u b q e", b=2, u=2, e=2)[:, :, :, cols(t, 32), :],
-                    sums[t, c0][:, cols(c - c0, QUARTER)].rearrange("p (b q u e) -> p u b q e", b=2, u=2, e=2),
-                )
+            for d0, d1 in z_turned:
+                if c0 <= d0 and d1 <= c1:
+                    nc.scalar.copy(
+                        z_turned[d0, d1][:].rearrange("p (b u q e) -> p u b q e", u=2, q=P, e=2)[:, :, :, cols(t, 32), :],
+                        sums[t, c0][:, (d0 - c0) * QUARTER : (d1 - c0) * QUARTER].rearrange(
+                            "p (b q u e) -> p u b q e", q=32, u=2, e=2
+                        ),
+                    )
 
         w4_w = tile("w4_w", [P, N], U32)
         w4_s = tile("w4_s", [P, N], U8)
 
-        w4_bf = [tile("w4_bf%d" % i, [P, N // 3, PACK], BF16) for i in range(3)]
-        for i in range(3):
-            round_and_interleave(w4_bf[i], w4_raw[:, :, cols(i, N // 3)])
+        w4_bf = tile("w4_bf", [P, N, PACK], BF16, tag="whole3")
+        for h in range(2):
+            round_and_interleave(w4_bf[:, cols(h, N // 2), :], w4_raw[:, :, cols(h, N // 2)])
         for t in range(SLICES - 1):
             surface(t, None)
         place_b(0)
@@ -258,12 +249,14 @@ def tile_list_occultation_humidity_score_kernel(
         open_sum(0, 0, 2, 0)
         larger(0, 0, 2, "sine1")
         place_b(2)
-        for i in range(3):
-            quantize(w4_w[:, cols(i, N // 3)], w4_s[:, cols(i, N // 3)], w4_bf[i][:].rearrange("p c i -> p (c i)"))
-        surface(3, "w4_bf2")
+        for h in range(2):
+            part = cols(h, N // 2)
+            quantize(w4_w[:, part], w4_s[:, part], w4_bf[:, part, :].rearrange("p c i -> p (c i)"))
+        surface(3, "whole3")
         open_sum(1, 0, 2, 1)
         larger(1, 0, 2, "wg2_t")
         open_sum(2, 0, 2, 0)
+        larger(2, 0, 2, "w4_raw")
         open_sum(3, 0, 1, 2)
         open_sum(3, 1, 2, 3)
         for t in range(SLICES):
@@ -275,7 +268,8 @@ def tile_list_occultation_humidity_score_kernel(
         z_in = {}
 
         def turn_back(c, b):
-            pairs = z_turned[c][:].bitcast(F32)
+            d0, d1 = [span for span in z_turned if span[0] <= c < span[1]][0]
+            pairs = z_turned[d0, d1][:].bitcast(F32)[:, cols(c - d0, BANK)]
             acc = bank("z_pairs%d" % c, b)
             for i in range(4):
                 nc.tensor.transpose(acc[:, cols(i)], pairs[:, cols(i)], ident[:])
@@ -300,13 +294,12 @@ def tile_list_occultation_humidity_score_kernel(
                 nc.vector.tensor_tensor(part, acc[:].rearrange("p (i m) -> p i m", i=2), part, ALU.mult)
                 nc.sync.dma_start(row_pair(out, n)[:, :, cols(c, QUARTER)], part)
 
-        larger(2, 0, 2, "sine3")
         larger(3, 0, 1)
         turn_back(0, 1)
         larger(3, 1, 2)
         turn_back(1, 0)
-        larger(0, 2, 4, "w4_bf2")
-        larger(1, 2, 4, "sine3")
+        larger(0, 2, 4, "sine3")
+        larger(1, 2, 4, "whole3")
         larger(2, 2, 4, "top3_0")
         larger(3, 2, 4)
         turn_back(2, 4)

@@ -161,7 +161,7 @@ def tile_list_occultation_humidity_score_kernel(
         quantize_w1(1)
         nc.vector.tensor_copy(v2_w[0][:], tab2_w[0][:].indirect(list2[:]))
         nc.vector.tensor_copy(v2_w[1][:], tab2_w[1][:].indirect(list2[:]))
-        page_a = [tile("page_a%d" % t, [P, T2], F32) for t in range(SLICES)]
+        page_a = [tile("page_a%d" % t, [P, T2], F32, tag="tab2_w1" if t == 0 else None) for t in range(SLICES)]
         page_b = [tile("page_b%d" % t, [P, T2], F32) for t in range(SLICES)]
         for page in page_a + page_b:
             nc.vector.memset(page[:].bitcast(I32), 0)

import math
from contextlib import ExitStack

import concourse.mybir as mybir
from concourse.masks import make_identity

F32 = mybir.dt.float32
BF16 = mybir.dt.bfloat16
I32 = mybir.dt.int32
U32 = mybir.dt.uint32
U16 = mybir.dt.uint16
U8 = mybir.dt.uint8
FP8X4 = mybir.dt.float8_e4m3fn_x4
FP4X4 = mybir.dt.float4_e2m1fn_x4
ACT = mybir.ActivationFunctionType
ALU = mybir.AluOpType

K, K2, H, N, T, TB, S, T2 = 512, 1024, 512, 768, 2048, 1024, 512, 1024
FLOPS = 2 * S * H * (K + 2 * K2) + 2 * H * N * T2

P = 128
PACK = 4
BANK = 512
SLICES = H // P
PASSES2 = K2 // (P * PACK)
QUARTER = T2 // 4
ROUNDER = 12582912.0


def tile_list_occultation_humidity_score_kernel(
    tc, tab_words, tab_scales, tab2_words, tab2_scales, offs, offs2, offs3, offs4, w1, g1,
    w2_words, w2_scales, w3_words, w3_scales, wg1, wg2, fc, w4, resid, out,
):
    nc = tc.nc
    with ExitStack() as ctx:
        sb = ctx.enter_context(tc.tile_pool(name="sb", bufs=1))
        ps = ctx.enter_context(tc.psum_pool(name="ps", bufs=1))

        def tile(name, shape, dtype, tag=None):
            return sb.tile(shape, dtype, name=name, tag=tag or name, align_bytes=64)

        def bank(name, b):
            return ps.tile([P, BANK], F32, name=name, tag="bank%d" % b)

        def cols(i, width=P):
            return slice(i * width, (i + 1) * width)

        def round_and_interleave(dst, src):
            nc.scalar.activation(
                dst.rearrange("p (c j) i -> p c i j", j=4),
                src.rearrange("p i (c j) -> p c i j", j=4),
                ACT.Copy,
            )

        def quantize(codes, scales, src):
            nc.vector.quantize_mx(out=codes.bitcast(FP8X4), scales=scales, in_=src)

        def add_transposed(dst, src, start, stop):
            nc.tensor.matmul(dst, lhsT=src, rhs=ident[:], is_transpose=True, start=start, stop=stop)

        tab_s = tile("tab_s", [P, T], U8)
        tab2_s = tile("tab2_s", [P, TB], U8)
        w2_s = tile("w2_s", [P, H], U8)
        w3_s = tile("w3_s", [P, PASSES2, H], U8)
        v2_s1 = tile("v2_s1", [P, S], U8)
        nc.vector.memset(tab2_s[:].bitcast(I32), 0)
        nc.vector.memset(w2_s[:].bitcast(I32), 0)
        nc.vector.memset(w3_s[:].rearrange("p a c -> p (a c)").bitcast(I32), 0)
        nc.vector.memset(v2_s1[:].bitcast(I32), 0)

        list1 = tile("list1", [P, S // 16], U16)
        list2 = tile("list2", [P, S // 16], U16)
        list3 = tile("list3", [P, S // 16], U16)
        list4 = tile("list4", [P, S // 16], U16)
        tab_w = tile("tab_w", [P, T], U32)
        tab2_w = [tile("tab2_w%d" % a, [P, TB], U32) for a in range(PASSES2)]
        w1_raw = [tile("w1_raw%d" % h, [P, PACK, H // 2], F32) for h in range(2)]
        w1_rows = w1.rearrange("(p i) c -> p i c", i=PACK)
        gain = tile("gain", [P, SLICES], F32)
        wg1_t = tile("wg1_t", [P, S], F32)
        wg2_t = tile("wg2_t", [P, S], F32)
        w2_w = tile("w2_w", [P, PASSES2, H], U32)
        w3_w = tile("w3_w", [P, PASSES2, 2 * H], U8)
        fc_t = [tile("fc_t%d" % t, [P, T2], F32) for t in range(SLICES)]
        w4_raw = tile("w4_raw", [P, PACK, N], F32)
        res = [tile("res%d" % n, [P, 2, T2], F32) for n in range(N // (2 * P))]

        def words(ap):
            return ap.rearrange("p t i -> p (t i)").bitcast(I32)

        def row_pair(ap, n):
            return ap[cols(n, 2 * P), :].rearrange("(i p) m -> p i m", p=P)

        nc.sync.dma_start(list1[:], offs)
        for q in range(4):
            rows = tab_scales[0, 4 * q : 4 * q + 4, :].bitcast(I32)
            nc.sync.dma_start(tab_s[32 * q : 32 * q + 32, :].bitcast(I32), rows.unsqueeze(0).broadcast_to([8, 4, T // 4]))
        nc.sync.dma_start(tab_w[:].bitcast(I32), words(tab_words[0]))
        nc.sync.dma_start(list2[:], offs2)
        nc.sync.dma_start(w1_raw[0][:], w1_rows[:, :, cols(0, H // 2)])
        for q in range(4):
            nc.sync.dma_start(tab2_s[32 * q : 32 * q + 8, :].bitcast(I32), tab2_scales[:, 4 * q : 4 * q + 4, :].bitcast(I32))
        nc.sync.dma_start(w1_raw[1][:], w1_rows[:, :, cols(1, H // 2)])
        with nc.allow_non_contiguous_dma(reason="one gain for each partition and slice"):
            nc.sync.dma_start(gain[:], g1.rearrange("(t p) -> p t", p=P))
        nc.sync.dma_start(wg1_t[:], wg1)
        nc.sync.dma_start(tab2_w[0][:].bitcast(I32), words(tab2_words[0]))
        nc.sync.dma_start(list3[:], offs3)
        nc.sync.dma_start(tab2_w[1][:].bitcast(I32), words(tab2_words[1]))
        nc.sync.dma_start(w2_w[:].bitcast(I32), w2_words.rearrange("a p c i -> p a (c i)").bitcast(I32))
        for q in range(4):
            nc.sync.dma_start(w2_s[32 * q : 32 * q + 8, :].bitcast(I32), w2_scales[:, 4 * q : 4 * q + 4, :].bitcast(I32))
        ident = tile("ident", [P, P], F32)
        make_identity(nc, ident[:])

        v_s = tile("v_s", [P, S], U8)
        v_w = tile("v_w", [P, S], U32)
        v2_s = tile("v2_s", [P, S], U8)
        v2_w = [tile("v2_w%d" % a, [P, S], U32) for a in range(PASSES2)]
        w1_bf = [tile("w1_bf%d" % h, [P, H // 2, PACK], BF16) for h in range(2)]
        w1_w = [tile("w1_w%d" % h, [P, H // 2], U32) for h in range(2)]
        w1_s = [tile("w1_s%d" % h, [P, H // 2], U8) for h in range(2)]
        gained = [tile("gained%d" % t, [P, S], F32) for t in range(SLICES)]
        tanh = [tile("tanh%d" % t, [P, S], F32) for t in range(SLICES)]

        def quantize_w1(h):
            round_and_interleave(w1_bf[h][:], w1_raw[h][:])
            quantize(w1_w[h][:], w1_s[h][:], w1_bf[h][:].rearrange("p c i -> p (c i)"))

        def bending(t):
            h, c = divmod(t, 2)
            acc = bank("h1_%d" % t, t)
            nc.tensor.matmul_mx(
                out=acc[:], lhsT=w1_w[h][:, cols(c)].bitcast(FP8X4), lhsT_scale=w1_s[h][:, cols(c)],
                rhs=v_w[:].bitcast(FP8X4), rhs_scale=v_s[:], start=True, stop=True,
            )
            nc.scalar.activation(gained[t][:], wg1_t[:], ACT.Copy, scale=gain[:, t : t + 1])
            nc.scalar.activation(tanh[t][:], acc[:], ACT.Tanh)

        def place_a(t):
            nc.vector.tensor_tensor(page_a[t][:].indirect(list3[:]), tanh[t][:], gained[t][:], ALU.mult)

        nc.vector.tensor_copy(v_s[:], tab_s[:].indirect(list1[:]))
        nc.vector.tensor_copy(v_w[:], tab_w[:].indirect(list1[:]))
        nc.vector.tensor_copy(v2_s[:], tab2_s[:].indirect(list2[:]))
        nc.sync.dma_start(w3_w[:].bitcast(I32), w3_words.rearrange("a p c -> p a c").bitcast(I32))
        nc.sync.dma_start(wg2_t[:], wg2)
        nc.sync.dma_start(list4[:], offs4)
        for q in range(4):
            nc.sync.dma_start(
                w3_s[32 * q : 32 * q + 4, :, :].bitcast(I32),
                w3_scales[:, 4 * q : 4 * q + 4, :].rearrange("a r c -> r a c").bitcast(I32),
            )
        nc.sync.dma_start(v2_s1[0:100, :].bitcast(I32), v2_s[4:104, :].bitcast(I32))
        nc.sync.dma_start(w4_raw[:], w4.rearrange("(p i) n -> p i n", i=PACK))
        for t in range(SLICES):
            nc.sync.dma_start(fc_t[t][:], fc[cols(t), :])
        for n in range(N // (2 * P)):
            nc.sync.dma_start(res[n][:], row_pair(resid, n))
        quantize_w1(0)
        quantize_w1(1)
        nc.vector.tensor_copy(v2_w[0][:], tab2_w[0][:].indirect(list2[:]))
        nc.vector.tensor_copy(v2_w[1][:], tab2_w[1][:].indirect(list2[:]))
        page_a = [tile("page_a%d" % t, [P, T2], F32, tag="tab2_w1" if t == 0 else None) for t in range(SLICES)]
        page_b = [tile("page_b%d" % t, [P, T2], F32) for t in range(SLICES)]
        for page in page_a + page_b:
            nc.vector.memset(page[:].bitcast(I32), 0)
        for t in range(SLICES):
            bending(t)
        place_a(0)
        place_a(1)

        turns = [tile("turns%d" % j, [P, H], F32) for j in range(S // P)]
        whole = [tile("whole%d" % j, [P, H], F32) for j in range(S // P)]
        frac = [bank("frac%d" % t, t) for t in range(SLICES)]
        phase = [bank("phase%d" % j, 4 + j) for j in range(S // P)]
        for j in range(S // P):
            for a in range(PASSES2):
                nc.tensor.matmul_mx(
                    out=phase[j][:], lhsT=v2_w[a][:, cols(j)].bitcast(FP8X4), lhsT_scale=v2_s[4 * a : P, cols(j)],
                    rhs=w2_w[:, a, :].bitcast(FP8X4), rhs_scale=w2_s[4 * a : P, :],
                    start=(a == 0), stop=(a == PASSES2 - 1),
                )
        for j in range(S // P):
            rounded = tile("rounded%d" % j, [P, H], U32, tag="rounded%d" % (j % 2))
            nc.scalar.activation(rounded[:], phase[j][:], ACT.Copy, scale=0.5 / math.pi, bias=ROUNDER)
            nc.scalar.activation(turns[j][:], phase[j][:], ACT.Copy, scale=0.5 / math.pi)
            nc.scalar.activation(whole[j][:], rounded[:], ACT.Copy, scale=-1.0, bias=ROUNDER)
            for t in range(SLICES):
                add_transposed(frac[t][:, cols(j)], turns[j][:, cols(t)], j == 0, False)
            for t in range(SLICES):
                add_transposed(frac[t][:, cols(j)], whole[j][:, cols(t)], False, j == S // P - 1)
        place_a(2)
        place_a(3)

        sine = [tile("sine%d" % t, [P, S], F32) for t in range(SLICES)]
        for t in range(SLICES):
            nc.scalar.activation(sine[t][:], frac[t][:], ACT.Sin, scale=2.0 * math.pi)

        weighted = {}

        def surface(t, tag):
            acc = bank("h3_%d" % t, 4 + t)
            for a in range(PASSES2):
                nc.tensor.matmul_mx(
                    out=acc[:], lhsT=w3_w[:, a, cols(t, 2 * P)].bitcast(FP4X4), lhsT_scale=w3_s[:, a, cols(t)],
                    rhs=v2_w[a][:].bitcast(FP8X4), rhs_scale=(v2_s, v2_s1)[a][:],
                    start=(a == 0), stop=(a == PASSES2 - 1),
                )
            weighted[t] = tile("weighted%d" % t, [P, S], F32, tag=tag)
            nc.vector.tensor_tensor(weighted[t][:], acc[:], wg2_t[:], ALU.mult)

        def place_b(t):
            nc.vector.tensor_tensor(page_b[t][:].indirect(list4[:]), sine[t][:], weighted[t][:], ALU.mult)

        z_turned = {(c0, c1): tile("z_turned%d" % c0, [P, (c1 - c0) * 2 * H], BF16) for c0, c1 in ((0, 1), (1, 2), (2, 4))}
        sums = {}

        def open_sum(t, c0, c1, b):
            sums[t, c0] = bank("sum%d_%d" % (t, c0), b)
            for i in range(2 * (c1 - c0)):
                add_transposed(sums[t, c0][:, cols(i)], fc_t[t][:, cols(2 * c0 + i)], i == 0, False)

        def larger(t, c0, c1, tag=None):
            levels = slice(c0 * QUARTER, c1 * QUARTER)
            top = tile("top%d_%d" % (t, c0), [P, (c1 - c0) * QUARTER], F32, tag=tag)
            nc.vector.tensor_tensor(top[:], page_a[t][:, levels], page_b[t][:, levels], ALU.max)
            for i in range(2 * (c1 - c0)):
                add_transposed(sums[t, c0][:, cols(i)], top[:, cols(i)], False, i == 2 * (c1 - c0) - 1)
            for d0, d1 in z_turned:
                if c0 <= d0 and d1 <= c1:
                    nc.scalar.copy(
                        z_turned[d0, d1][:].rearrange("p (b u q e) -> p u b q e", u=2, q=P, e=2)[:, :, :, cols(t, 32), :],
                        sums[t, c0][:, (d0 - c0) * QUARTER : (d1 - c0) * QUARTER].rearrange(
                            "p (b q u e) -> p u b q e", q=32, u=2, e=2
                        ),
                    )

        w4_w = tile("w4_w", [P, N], U32)
        w4_s = tile("w4_s", [P, N], U8)

        w4_bf = tile("w4_bf", [P, N, PACK], BF16, tag="whole3")
        for h in range(2):
            round_and_interleave(w4_bf[:, cols(h, N // 2), :], w4_raw[:, :, cols(h, N // 2)])
        for t in range(SLICES - 1):
            surface(t, None)
        place_b(0)
        place_b(1)
        open_sum(0, 0, 2, 0)
        larger(0, 0, 2, "sine1")
        place_b(2)
        for h in range(2):
            part = cols(h, N // 2)
            quantize(w4_w[:, part], w4_s[:, part], w4_bf[:, part, :].rearrange("p c i -> p (c i)"))
        surface(3, "whole3")
        open_sum(1, 0, 2, 1)
        larger(1, 0, 2, "wg2_t")
        open_sum(2, 0, 2, 0)
        larger(2, 0, 2, "w4_raw")
        open_sum(3, 0, 1, 2)
        open_sum(3, 1, 2, 3)
        for t in range(SLICES):
            open_sum(t, 2, 4, 4 + t)
        place_b(3)

        z_w = [tile("z_w%d" % c, [P, QUARTER], U32) for c in range(4)]
        z_s = [tile("z_s%d" % c, [P, QUARTER], U8) for c in range(4)]
        z_in = {}

        def turn_back(c, b):
            d0, d1 = [span for span in z_turned if span[0] <= c < span[1]][0]
            pairs = z_turned[d0, d1][:].bitcast(F32)[:, cols(c - d0, BANK)]
            acc = bank("z_pairs%d" % c, b)
            for i in range(4):
                nc.tensor.transpose(acc[:, cols(i)], pairs[:, cols(i)], ident[:])
            z_in[c] = tile("z_in%d" % c, [P, QUARTER * PACK], BF16)
            nc.scalar.copy(
                z_in[c][:].bitcast(F32).rearrange("p (b m u) -> p b m u", b=2, u=2),
                acc[:].rearrange("p (b u m) -> p b m u", b=2, u=2),
            )

        score_banks = (2, 3, 1, 0, 6, 7, 2, 3, 1, 0, 4, 5)

        def score(c):
            for n in range(N // (2 * P)):
                acc = bank("y%d_%d" % (c, n), score_banks[3 * c + n])
                for i in range(2):
                    nc.tensor.matmul_mx(
                        out=acc[:, cols(i, QUARTER)], lhsT=w4_w[:, cols(2 * n + i)].bitcast(FP8X4),
                        lhsT_scale=w4_s[:, cols(2 * n + i)],
                        rhs=z_w[c][:].bitcast(FP8X4), rhs_scale=z_s[c][:], start=True, stop=True,
                    )
                part = res[n][:, :, cols(c, QUARTER)]
                nc.vector.tensor_tensor(part, acc[:].rearrange("p (i m) -> p i m", i=2), part, ALU.mult)
                nc.sync.dma_start(row_pair(out, n)[:, :, cols(c, QUARTER)], part)

        larger(3, 0, 1)
        turn_back(0, 1)
        larger(3, 1, 2)
        turn_back(1, 0)
        larger(0, 2, 4, "sine3")
        larger(1, 2, 4, "whole3")
        larger(2, 2, 4, "top3_0")
        larger(3, 2, 4)
        turn_back(2, 4)
        turn_back(3, 5)
        quantize(z_w[0][:], z_s[0][:], z_in[0][:])
        for c in range(4):
            if c + 1 < 4:
                quantize(z_w[c + 1][:], z_s[c + 1][:], z_in[c + 1][:])
            score(c)
